import numpy as np
import ml_dtypes


def mxq(x, axis, fmt="e4m3"):
    dtype, down = {"e4m3": (ml_dtypes.float8_e4m3fn, 7), "e5m2": (ml_dtypes.float8_e5m2, 14)}[fmt]
    v = np.moveaxis(np.asarray(x, np.float32).astype(ml_dtypes.bfloat16).astype(np.float64), axis, -1)
    blocks = v.reshape(v.shape[:-1] + (-1, 32))
    amax = np.abs(blocks).max(-1, keepdims=True)
    byte = np.maximum(np.where(amax > 0, np.frexp(amax)[1] - 1 + 127, 0) - down, 1)
    scale = np.exp2(byte - 127.0)
    codes = (blocks / scale).astype(np.float32).astype(dtype).astype(np.float64)
    return np.moveaxis((codes * scale).reshape(v.shape), -1, axis)


WIDE = False


def mx_kscale(k):
    if not WIDE:
        return np.ones(k)
    levels = np.array([10, -10, 5, -5, 0])
    if k % 512:
        return np.exp2(np.random.permutation(np.resize(levels, k // 32))).repeat(32)
    a = np.empty((k // 512, 16))
    for p in range(k // 512):
        a[p, :8] = np.random.permutation(np.resize(levels, 8))
        for g in range(8):
            far = levels[np.abs(levels - a[p, g]) >= 10]
            a[p, g + 8] = far[np.random.randint(len(far))]
    return np.exp2(a.ravel()).repeat(32)


def f64(x):
    return np.asarray(x).astype(np.float64)


def striped(idx):
    return np.tile(np.asarray(idx).reshape(-1, 16).T, (8, 1)).astype(np.uint16)


def unstriped(offs):
    return offs[:16].T.reshape(-1).astype(np.int64)


E2M1 = np.array([0.0, 0.5, 1.0, 1.5, 2.0, 3.0, 4.0, 6.0, -0.0, -0.5, -1.0, -1.5, -2.0, -3.0, -4.0, -6.0])


def pack_weight(w, fmt):
    k, n = w.shape
    w = f64(np.asarray(w, np.float32).astype(ml_dtypes.bfloat16)).reshape(k // 32, 32, n)
    amax = np.abs(w).max(1)
    if fmt == "e4m3":
        byte = np.frexp(amax)[1] - 1 + 127 - 7
    else:
        mant, ex = np.frexp(amax / 6.0)
        byte = np.where(mant > 0.5, ex, ex - 1) + 127
    byte = np.clip(np.where(amax > 0, byte, 1), 1, 254)
    scaled = (w * np.exp2(127.0 - byte)[:, None, :]).reshape(k, n).astype(np.float32)
    by_word = np.ascontiguousarray(scaled.reshape(k // 512, 128, 4, n).transpose(0, 1, 3, 2))
    if fmt == "e4m3":
        words = by_word.astype(ml_dtypes.float8_e4m3fn).view(np.uint8)
    else:
        c = by_word.astype(ml_dtypes.float4_e2m1fn).view(np.uint8) & 0xF
        words = (c[..., 0::2] | (c[..., 1::2] << 4)).reshape(k // 512, 128, 2 * n)
    return np.ascontiguousarray(words), np.ascontiguousarray(byte.astype(np.uint8).reshape(k // 512, 16, n))


def unpack_weight(words, scales, fmt):
    g, _, n = scales.shape
    words = np.ascontiguousarray(words).reshape(g, 128, n, -1)
    if fmt == "e4m3":
        vals = words.view(ml_dtypes.float8_e4m3fn).astype(np.float64)
    else:
        nib = np.empty((g, 128, n, 4), np.uint8)
        nib[..., 0::2] = words & 0xF
        nib[..., 1::2] = words >> 4
        vals = E2M1[nib]
    vals = vals * np.repeat(np.exp2(scales.astype(np.float64) - 127.0), 8, axis=1)[..., None]
    return vals.transpose(0, 1, 3, 2).reshape(g * 512, n)


def bf(x):
    return np.asarray(x, np.float32).astype(ml_dtypes.bfloat16)


def planes(Y):
    r, m = Y.shape
    b = f64(bf(Y)).reshape(r // 32, 32, m)
    amax = np.abs(b).max(1)
    byte = np.clip(np.where(amax > 0, np.frexp(amax)[1] - 1 + 127 - 7, 1), 1, 254)
    codes = (b * np.exp2(127.0 - byte)[:, None, :]).reshape(r, m).astype(np.float32).astype(ml_dtypes.float8_e4m3fn).view(np.uint8)
    words = codes.reshape(r // 512, 128, 4, m).transpose(0, 1, 3, 2)
    return np.ascontiguousarray(words), np.ascontiguousarray(byte.astype(np.uint8).reshape(r // 512, 16, m))


D, T, I, Q, E, G = 512, 2048, 512, 256, 512, 64


def setup_inputs():
    n = np.random.standard_normal
    idx = np.random.permutation(T)[:I]
    fd = mx_kscale(D)
    fi = mx_kscale(I)
    ti = np.ones(T)
    ti[idx] = fi
    keysp = pack_weight(n((D, T)) / fd[:, None], "e2m1")
    return {
        "query": (n((D, Q)) * 0.5 / np.sqrt(D) * fd[:, None]).astype(np.float32),
        "keys_words": keysp[0],
        "keys_scales": keysp[1],
        "sharp": (np.random.uniform(0.5, 2.0, (Q, 1))).astype(np.float32),
        "size": (np.random.uniform(0.5, 2.0, (1, I)) * fi).astype(np.float32),
        "vals": (n((E, T)) / ti).astype(np.float32),
        "offs": striped(idx),
    }


def reference(query, keys_words, keys_scales, sharp, size, vals, offs):
    idx = unstriped(offs)
    keysu = unpack_weight(keys_words, keys_scales, "e2m1")
    queryq = mxq(f64(query), 0, "e4m3")
    keysidxg = keysu[:, idx]
    a = queryq.T @ keysidxg
    b = a.reshape(Q, G, I // G).max(axis=2)
    br = np.repeat(b, I // G, axis=1)
    p = np.exp((a - br) * f64(sharp)) * np.exp(br - np.max(br, axis=1, keepdims=True))
    w = p * f64(size) / np.sum(p, axis=1, keepdims=True)
    wt = w.T
    vt = f64(vals)[:, idx].T
    vtq = mxq(vt, 0, "e4m3")
    wtq = mxq(wt, 0, "e4m3")
    o = vtq.T @ wtq
    words, scales = planes(o)
    return o, words, scales

@@ -1,0 +1,188 @@
+from contextlib import ExitStack
+
+import concourse.mybir as mybir
+from concourse.masks import make_identity
+
+D, T, I, Q, E, G = 512, 2048, 512, 256, 512, 64
+FLOPS = 2 * D * Q * I + 2 * I * E * Q
+
+F32 = mybir.dt.float32
+BF16 = mybir.dt.bfloat16
+I32 = mybir.dt.int32
+U32 = mybir.dt.uint32
+U16 = mybir.dt.uint16
+U8 = mybir.dt.uint8
+FP8X4 = mybir.dt.float8_e4m3fn_x4
+FP4X4 = mybir.dt.float4_e2m1fn_x4
+ALU = mybir.AluOpType
+ACT = mybir.ActivationFunctionType
+AX = mybir.AxisListType
+
+P = 128
+PACK = 4
+HALVES = Q // P
+GROUP = I // G
+
+
+def tile_attend_nearbest_pl_kernel(tc, query, keys_words, keys_scales, sharp, size, vals, offs, out_0, out_1, out_2):
+    nc = tc.nc
+    with ExitStack() as ctx:
+        sb = ctx.enter_context(tc.tile_pool(name="sb", bufs=1))
+        ps = ctx.enter_context(tc.psum_pool(name="ps", bufs=1))
+
+        def alloc(name, shape, dtype, tag=None):
+            return sb.tile(shape, dtype, name=name, tag=tag or name, align_bytes=64)
+
+        offsets = sb.tile([P, I // 16], U16, name="offsets")
+        nc.sync.dma_start(offsets[:], offs)
+        key_scale_pool = alloc("key_scale_pool", [P, T], U8)
+        nc.gpsimd.memset(key_scale_pool[:].bitcast(I32), 0)
+        key_word_pool = alloc("key_word_pool", [P, T], U16)
+        nc.sync.dma_start(key_word_pool[:].bitcast(I32), keys_words[0].bitcast(I32))
+        for quad in range(4):
+            nc.sync.dma_start(
+                key_scale_pool[32 * quad : 32 * quad + 4, :].bitcast(I32),
+                keys_scales[0, 4 * quad : 4 * quad + 4, :].bitcast(I32),
+            )
+        q_raw = alloc("q_raw", [P, PACK, Q], F32)
+        nc.sync.dma_start(q_raw[:], query.rearrange("(p t) q -> p t q", t=PACK))
+        val_rows = vals.rearrange("(p t) n -> t p n", t=PACK)
+        val_pool = [alloc("val_pool%d" % t, [P, T], F32) for t in range(PACK)]
+        sharp_sb = alloc("sharp_sb", [P, HALVES], F32)
+        with nc.allow_non_contiguous_dma(reason="one value a partition"):
+            nc.sync.dma_start(sharp_sb[:], sharp.rearrange("(h p) o -> p (h o)", p=P))
+        nc.sync.dma_start(val_pool[0][:], val_rows[0])
+        size_sb = alloc("size_sb", [P, PACK], F32)
+        nc.sync.dma_start(size_sb[:], size.rearrange("o (p t) -> p (o t)", t=PACK))
+        for t in range(1, PACK):
+            nc.sync.dma_start(val_pool[t][:], val_rows[t])
+
+        ident = alloc("ident", [P, P], F32)
+        make_identity(nc, ident[:])
+        warm = alloc("warm", [P, 1], F32)
+        nc.vector.memset(warm[:], 0.0)
+        warm_out = alloc("warm_out", [P, 1], F32)
+        nc.scalar.activation(warm_out[:], warm[:], ACT.Exp)
+        one_less = alloc("one_less", [P, HALVES], F32)
+        nc.gpsimd.tensor_scalar(one_less[:], sharp_sb[:], -1.0, 1.0, ALU.mult, ALU.add)
+
+        size_rows = ps.tile([P, PACK, P], F32, name="size_rows")
+        for t in range(PACK):
+            nc.tensor.transpose(size_rows[:, t, :], size_sb[:, t : t + 1].to_broadcast([P, P]), ident[:])
+
+        key_words = alloc("key_words", [P, I], U16)
+        nc.vector.tensor_copy(key_words[:], key_word_pool[:].indirect(offsets[:]))
+        key_scales = alloc("key_scales", [P, I], U8)
+        nc.vector.tensor_copy(key_scales[:], key_scale_pool[:].indirect(offsets[:]))
+
+        q_bf = alloc("q_bf", [P, Q, PACK], BF16)
+        nc.scalar.copy(q_bf[:].rearrange("p (c j) t -> p c t j", j=4), q_raw[:].rearrange("p t (c j) -> p c t j", j=4))
+        q_codes = alloc("q_codes", [P, Q], U32)
+        q_scales = alloc("q_scales", [P, Q], U8)
+        nc.vector.quantize_mx(q_codes[:].bitcast(FP8X4), q_scales[:], q_bf[:].rearrange("p c t -> p (c t)"))
+        scores = []
+        for h in range(HALVES):
+            cols = slice(h * P, (h + 1) * P)
+            a = ps.tile([P, I], F32, name="a%d" % h, tag="a%d" % h)
+            nc.tensor.matmul_mx(
+                a[:], lhsT=q_codes[:, cols].bitcast(FP8X4), lhsT_scale=q_scales[:, cols],
+                rhs=key_words[:].bitcast(FP4X4), rhs_scale=key_scales[:], start=True, stop=True,
+            )
+            scores.append(a)
+        val0_bf = alloc("val0_bf", [P, T], BF16)
+        nc.scalar.activation(val0_bf[:], val_pool[0][:], ACT.Copy)
+
+        best = alloc("best", [P, HALVES, G], F32)
+        shift = [alloc("shift%d" % h, [P, G], F32) for h in range(HALVES)]
+        neg_top = alloc("neg_top", [P, HALVES], F32)
+        expo = [alloc("expo%d" % h, [P, G, GROUP], F32) for h in range(HALVES)]
+        prob = [alloc("prob%d" % h, [P, I], F32) for h in range(HALVES)]
+        total = [alloc("total%d" % h, [P, 1], F32) for h in range(HALVES)]
+        inv = [alloc("inv%d" % h, [P, 1], F32) for h in range(HALVES)]
+        for h in range(HALVES):
+            nc.vector.tensor_reduce(best[:, h, :], scores[h][:].rearrange("p (g j) -> p g j", j=GROUP), AX.X, ALU.max)
+        for h in range(HALVES):
+            nc.gpsimd.tensor_scalar(shift[h][:], best[:, h, :], one_less[:, h : h + 1], 0.0, ALU.mult, ALU.add)
+        for h in range(HALVES):
+            nc.vector.scalar_tensor_tensor(
+                expo[h][:], scores[h][:].rearrange("p (g j) -> p g j", j=GROUP), sharp_sb[:, h : h + 1],
+                shift[h][:].unsqueeze(2).to_broadcast([P, G, GROUP]), ALU.mult, ALU.add,
+            )
+            if h == 0:
+                nc.vector.tensor_reduce(neg_top[:], best[:], AX.X, ALU.max, negate=True)
+            nc.scalar.activation(
+                prob[h][:], expo[h][:].rearrange("p g j -> p (g j)"), ACT.Exp, bias=neg_top[:, h : h + 1], accum_out=total[h][:]
+            )
+
+
+        def turn(grouped, rows_bf, bank):
+            words = rows_bf[:].bitcast(F32)
+            for u in range(2):
+                nc.tensor.transpose(bank[:, u, :], words[:, u : I // 2 : 2], ident[:])
+            nc.scalar.copy(grouped.bitcast(F32).rearrange("p (r u) -> p r u", u=2), bank[:, 0:2, :].rearrange("p u r -> p r u"))
+
+        def quantize(name, grouped, blocks, tag=None):
+            codes = alloc(name + "_codes", [P, blocks * P], U32, tag)
+            scales = alloc(name + "_scales", [P, blocks * P], U8)
+            nc.vector.quantize_mx(codes[:].bitcast(FP8X4), scales[:], grouped)
+            return [(codes[:, b * P : (b + 1) * P].bitcast(FP8X4), scales[:, b * P : (b + 1) * P]) for b in range(blocks)]
+
+        def gather_values(t, grouped):
+            v_bf = alloc("v_bf%d" % t, [P, I], BF16)
+            if t == 0:
+                nc.scalar.activation(v_bf[:], val0_bf[:].indirect(offsets[:]), ACT.Copy)
+            else:
+                nc.vector.tensor_copy(v_bf[:], val_pool[t][:].indirect(offsets[:]))
+            bank = ps.tile([P, PACK, P], F32, name="v_bank", tag="v_bank", bufs=2)
+            turn(grouped, v_bf, bank)
+
+        early = alloc("early", [P, 4 * I], BF16)
+        late = [alloc("late%d" % t, [P, I], BF16) for t in (2, 3)]
+        gather_values(1, early[:, 3 * I : 4 * I])
+        gather_values(0, early[:, 2 * I : 3 * I])
+        for h in range(HALVES):
+            nc.vector.reciprocal(inv[h][:], total[h][:])
+            w_bf = alloc("w_bf%d" % h, [P, I], BF16)
+            nc.vector.scalar_tensor_tensor(
+                w_bf[:].rearrange("p (n t) -> p n t", t=PACK), prob[h][:].rearrange("p (n t) -> p n t", t=PACK), inv[h][:],
+                size_rows[:].rearrange("p t n -> p n t"), ALU.mult, ALU.mult,
+            )
+            bank = ps.tile([P, PACK, P], F32, name="w_bank", tag="a%d" % h)
+            turn(early[:, h * I : (h + 1) * I], w_bf, bank)
+        gather_values(2, late[0][:])
+        operands = quantize("early", early[:], 4, "val_pool2")
+        weights, values = operands[:2], operands[2:]
+        gather_values(3, late[1][:])
+        values = values + quantize("v2", late[0][:], 1, "val_pool3") + quantize("v3", late[1][:], 1)
+
+        result = [ps.tile([P, PACK, P], F32, name="result%d" % h) for h in range(HALVES)]
+        y = alloc("y", [P, PACK, Q], F32)
+        out_rows = out_0.rearrange("(p t) q -> p t q", t=PACK)
+        y_bf = [alloc("y_bf%d" % h, [P, P, PACK], BF16) for h in range(HALVES)]
+        y_codes = alloc("y_codes", [P, Q], U32)
+        y_scales = alloc("y_scales", [P, Q], U8)
+        for planes in ((0, 1), (2, 3)):
+            for t in planes:
+                for h in range(HALVES):
+                    nc.tensor.matmul_mx(
+                        result[h][:, t, :], lhsT=values[t][0], lhsT_scale=values[t][1],
+                        rhs=weights[h][0], rhs_scale=weights[h][1], start=True, stop=True,
+                    )
+            if planes[0] == 0:
+                rows = slice(planes[0], planes[-1] + 1)
+                for h in range(HALVES):
+                    nc.scalar.copy(y[:, rows, h * P : (h + 1) * P], result[h][:, rows, :])
+                nc.sync.dma_start(out_rows[:, rows, :], y[:, rows, :])
+        last = slice(2, PACK)
+        nc.vector.tensor_copy(y_bf[0][:], result[0][:].rearrange("p t q -> p q t"))
+        nc.scalar.copy(y_bf[1][:], result[1][:].rearrange("p t q -> p q t"))
+        nc.vector.tensor_copy(y[:, last, 0:P], result[0][:, last, :])
+        nc.scalar.copy(y[:, last, P:Q], result[1][:, last, :])
+        for h in range(HALVES):
+            cols = slice(h * P, (h + 1) * P)
+            nc.vector.quantize_mx(y_codes[:, cols].bitcast(FP8X4), y_scales[:, cols], y_bf[h][:].rearrange("p q t -> p (q t)"))
+        nc.scalar.dma_start(out_rows[:, last, :], y[:, last, :])
+        nc.sync.dma_start(out_1[0].rearrange("p c r -> p (c r)").bitcast(I32), y_codes[:].bitcast(I32))
+        for quad in range(4):
+            queue = nc.sync if quad % 2 else nc.scalar
+            queue.dma_start(out_2[0, 4 * quad : 4 * quad + 4, :].bitcast(I32), y_scales[32 * quad : 32 * quad + 4, :].bitcast(I32))

@@ -36,7 +36,8 @@ def tile_attend_nearbest_pl_kernel(tc, query, keys_words, keys_scales, sharp, si
         offsets = sb.tile([P, I // 16], U16, name="offsets")
         nc.sync.dma_start(offsets[:], offs)
         key_scale_pool = alloc("key_scale_pool", [P, T], U8)
-        nc.gpsimd.memset(key_scale_pool[:].bitcast(I32), 0)
+        nc.gpsimd.memset(key_scale_pool[:, : T // 2].bitcast(I32), 0)
+        nc.vector.memset(key_scale_pool[:, T // 2 :].bitcast(I32), 0)
         key_word_pool = alloc("key_word_pool", [P, T], U16)
         nc.sync.dma_start(key_word_pool[:].bitcast(I32), keys_words[0].bitcast(I32))
         for quad in range(4):
@@ -66,7 +67,7 @@ def tile_attend_nearbest_pl_kernel(tc, query, keys_words, keys_scales, sharp, si
         one_less = alloc("one_less", [P, HALVES], F32)
         nc.gpsimd.tensor_scalar(one_less[:], sharp_sb[:], -1.0, 1.0, ALU.mult, ALU.add)
 
-        size_rows = ps.tile([P, PACK, P], F32, name="size_rows")
+        size_rows = ps.tile([P, PACK, P], F32, name="size_rows", tag="size_rows")
         for t in range(PACK):
             nc.tensor.transpose(size_rows[:, t, :], size_sb[:, t : t + 1].to_broadcast([P, P]), ident[:])
 
@@ -75,14 +76,19 @@ def tile_attend_nearbest_pl_kernel(tc, query, keys_words, keys_scales, sharp, si
         key_scales = alloc("key_scales", [P, I], U8)
         nc.vector.tensor_copy(key_scales[:], key_scale_pool[:].indirect(offsets[:]))
 
-        q_bf = alloc("q_bf", [P, Q, PACK], BF16)
-        nc.scalar.copy(q_bf[:].rearrange("p (c j) t -> p c t j", j=4), q_raw[:].rearrange("p t (c j) -> p c t j", j=4))
+        copy_out = (nc.vector.tensor_copy, nc.scalar.copy)
+        q_bf = [alloc("q_bf%d" % h, [P, P, PACK], BF16) for h in range(HALVES)]
+        for h in range(HALVES):
+            nc.scalar.copy(
+                q_bf[h][:].rearrange("p (c j) t -> p c t j", j=4),
+                q_raw[:, :, h * P : (h + 1) * P].rearrange("p t (c j) -> p c t j", j=4),
+            )
         q_codes = alloc("q_codes", [P, Q], U32)
         q_scales = alloc("q_scales", [P, Q], U8)
-        nc.vector.quantize_mx(q_codes[:].bitcast(FP8X4), q_scales[:], q_bf[:].rearrange("p c t -> p (c t)"))
         scores = []
         for h in range(HALVES):
             cols = slice(h * P, (h + 1) * P)
+            nc.vector.quantize_mx(q_codes[:, cols].bitcast(FP8X4), q_scales[:, cols], q_bf[h][:].rearrange("p c t -> p (c t)"))
             a = ps.tile([P, I], F32, name="a%d" % h, tag="a%d" % h)
             nc.tensor.matmul_mx(
                 a[:], lhsT=q_codes[:, cols].bitcast(FP8X4), lhsT_scale=q_scales[:, cols],
@@ -121,27 +127,24 @@ def tile_attend_nearbest_pl_kernel(tc, query, keys_words, keys_scales, sharp, si
                 nc.tensor.transpose(bank[:, u, :], words[:, u : I // 2 : 2], ident[:])
             nc.scalar.copy(grouped.bitcast(F32).rearrange("p (r u) -> p r u", u=2), bank[:, 0:2, :].rearrange("p u r -> p r u"))
 
-        def quantize(name, grouped, blocks, tag=None):
-            codes = alloc(name + "_codes", [P, blocks * P], U32, tag)
-            scales = alloc(name + "_scales", [P, blocks * P], U8)
-            nc.vector.quantize_mx(codes[:].bitcast(FP8X4), scales[:], grouped)
-            return [(codes[:, b * P : (b + 1) * P].bitcast(FP8X4), scales[:, b * P : (b + 1) * P]) for b in range(blocks)]
-
-        def gather_values(t, grouped):
-            v_bf = alloc("v_bf%d" % t, [P, I], BF16)
+        def gather_values(t):
+            v_bf = alloc("v_bf%d" % t, [P, I], BF16, ("expo1", "shift1", "prob1", "val_pool2")[t])
             if t == 0:
                 nc.scalar.activation(v_bf[:], val0_bf[:].indirect(offsets[:]), ACT.Copy)
             else:
                 nc.vector.tensor_copy(v_bf[:], val_pool[t][:].indirect(offsets[:]))
-            bank = ps.tile([P, PACK, P], F32, name="v_bank", tag="v_bank", bufs=2)
-            turn(grouped, v_bf, bank)
+            return v_bf
 
-        early = alloc("early", [P, 4 * I], BF16)
+        def turn_values(grouped, v_bf):
+            turn(grouped, v_bf, ps.tile([P, PACK, P], F32, name="v_bank", tag="v_bank", bufs=2))
+
+        first_values = gather_values(0)
+        early = alloc("early", [P, 4 * I], BF16, "val0_bf")
         late = [alloc("late%d" % t, [P, I], BF16) for t in (2, 3)]
-        gather_values(1, early[:, 3 * I : 4 * I])
-        gather_values(0, early[:, 2 * I : 3 * I])
+        turn_values(early[:, 3 * I : 4 * I], gather_values(1))
         for h in range(HALVES):
             nc.vector.reciprocal(inv[h][:], total[h][:])
+        for h in range(HALVES):
             w_bf = alloc("w_bf%d" % h, [P, I], BF16)
             nc.vector.scalar_tensor_tensor(
                 w_bf[:].rearrange("p (n t) -> p n t", t=PACK), prob[h][:].rearrange("p (n t) -> p n t", t=PACK), inv[h][:],
@@ -149,39 +152,41 @@ def tile_attend_nearbest_pl_kernel(tc, query, keys_words, keys_scales, sharp, si
             )
             bank = ps.tile([P, PACK, P], F32, name="w_bank", tag="a%d" % h)
             turn(early[:, h * I : (h + 1) * I], w_bf, bank)
-        gather_values(2, late[0][:])
-        operands = quantize("early", early[:], 4, "val_pool2")
-        weights, values = operands[:2], operands[2:]
-        gather_values(3, late[1][:])
-        values = values + quantize("v2", late[0][:], 1, "val_pool3") + quantize("v3", late[1][:], 1)
+        turn(early[:, 2 * I : 3 * I], first_values, ps.tile([P, PACK, P], F32, name="v0_bank", tag="size_rows"))
+        turn_values(late[0][:], gather_values(2))
+        turn_values(late[1][:], gather_values(3))
+        codes = alloc("codes", [P, 6 * P], U32, "val_pool3")
+        scales = alloc("scales", [P, 6 * P], U8)
+        for first, grouped in ((0, early), (4, late[0]), (5, late[1])):
+            cols = slice(first * P, first * P + grouped.shape[1] // PACK)
+            nc.vector.quantize_mx(codes[:, cols].bitcast(FP8X4), scales[:, cols], grouped[:])
+        w_codes, w_scales = codes[:, :Q].bitcast(FP8X4), scales[:, :Q]
 
-        result = [ps.tile([P, PACK, P], F32, name="result%d" % h) for h in range(HALVES)]
         y = alloc("y", [P, PACK, Q], F32)
         out_rows = out_0.rearrange("(p t) q -> p t q", t=PACK)
-        y_bf = [alloc("y_bf%d" % h, [P, P, PACK], BF16) for h in range(HALVES)]
+        for rows, copy in ((slice(0, 2), nc.scalar.copy), (slice(2, 3), nc.vector.tensor_copy), (slice(3, 4), nc.scalar.copy)):
+            result = ps.tile([P, rows.stop - rows.start, Q], F32, name="result%d" % rows.start)
+            for t in range(rows.start, rows.stop):
+                cols = slice(Q + t * P, Q + (t + 1) * P)
+                nc.tensor.matmul_mx(
+                    result[:, t - rows.start, :], lhsT=codes[:, cols].bitcast(FP8X4), lhsT_scale=scales[:, cols],
+                    rhs=w_codes, rhs_scale=w_scales, start=True, stop=True,
+                )
+            copy(y[:, rows, :], result[:])
+            if rows.start != 2:
+                stored = slice(0, 2) if rows.start == 0 else slice(2, 4)
+                nc.sync.dma_start(out_rows[:, stored, :], y[:, stored, :])
         y_codes = alloc("y_codes", [P, Q], U32)
         y_scales = alloc("y_scales", [P, Q], U8)
-        for planes in ((0, 1), (2, 3)):
-            for t in planes:
-                for h in range(HALVES):
-                    nc.tensor.matmul_mx(
-                        result[h][:, t, :], lhsT=values[t][0], lhsT_scale=values[t][1],
-                        rhs=weights[h][0], rhs_scale=weights[h][1], start=True, stop=True,
-                    )
-            if planes[0] == 0:
-                rows = slice(planes[0], planes[-1] + 1)
-                for h in range(HALVES):
-                    nc.scalar.copy(y[:, rows, h * P : (h + 1) * P], result[h][:, rows, :])
-                nc.sync.dma_start(out_rows[:, rows, :], y[:, rows, :])
-        last = slice(2, PACK)
-        nc.vector.tensor_copy(y_bf[0][:], result[0][:].rearrange("p t q -> p q t"))
-        nc.scalar.copy(y_bf[1][:], result[1][:].rearrange("p t q -> p q t"))
-        nc.vector.tensor_copy(y[:, last, 0:P], result[0][:, last, :])
-        nc.scalar.copy(y[:, last, P:Q], result[1][:, last, :])
+        y_bf = [alloc("y_bf%d" % h, [P, P, PACK], BF16) for h in range(HALVES)]
+        for h in range(HALVES):
+            copy_out[h](
+                y_bf[h][:].rearrange("p (c j) t -> p c t j", j=4),
+                y[:, :, h * P : (h + 1) * P].rearrange("p t (c j) -> p c t j", j=4),
+            )
         for h in range(HALVES):
             cols = slice(h * P, (h + 1) * P)
             nc.vector.quantize_mx(y_codes[:, cols].bitcast(FP8X4), y_scales[:, cols], y_bf[h][:].rearrange("p q t -> p (q t)"))
-        nc.scalar.dma_start(out_rows[:, last, :], y[:, last, :])
         nc.sync.dma_start(out_1[0].rearrange("p c r -> p (c r)").bitcast(I32), y_codes[:].bitcast(I32))
         for quad in range(4):
             queue = nc.sync if quad % 2 else nc.scalar

@@ -50,8 +50,7 @@ def tile_attend_nearbest_pl_kernel(tc, query, keys_words, keys_scales, sharp, si
         val_rows = vals.rearrange("(p t) n -> t p n", t=PACK)
         val_pool = [alloc("val_pool%d" % t, [P, T], F32) for t in range(PACK)]
         sharp_sb = alloc("sharp_sb", [P, HALVES], F32)
-        with nc.allow_non_contiguous_dma(reason="one value a partition"):
-            nc.sync.dma_start(sharp_sb[:], sharp.rearrange("(h p) o -> p (h o)", p=P))
+        nc.sync.dma_start(sharp_sb[:], sharp.rearrange("(p h) o -> p (h o)", h=HALVES))
         nc.sync.dma_start(val_pool[0][:], val_rows[0])
         size_sb = alloc("size_sb", [P, PACK], F32)
         nc.sync.dma_start(size_sb[:], size.rearrange("o (p t) -> p (o t)", t=PACK))
@@ -80,8 +79,8 @@ def tile_attend_nearbest_pl_kernel(tc, query, keys_words, keys_scales, sharp, si
         q_bf = [alloc("q_bf%d" % h, [P, P, PACK], BF16) for h in range(HALVES)]
         for h in range(HALVES):
             nc.scalar.copy(
-                q_bf[h][:].rearrange("p (c j) t -> p c t j", j=4),
-                q_raw[:, :, h * P : (h + 1) * P].rearrange("p t (c j) -> p c t j", j=4),
+                q_bf[h][:].rearrange("p (c j) t -> p c t j", j=2),
+                q_raw[:].rearrange("p t (c j h) -> p h c t j", j=2, h=HALVES)[:, h],
             )
         q_codes = alloc("q_codes", [P, Q], U32)
         q_scales = alloc("q_scales", [P, Q], U8)
@@ -172,7 +171,7 @@ def tile_attend_nearbest_pl_kernel(tc, query, keys_words, keys_scales, sharp, si
                     result[:, t - rows.start, :], lhsT=codes[:, cols].bitcast(FP8X4), lhsT_scale=scales[:, cols],
                     rhs=w_codes, rhs_scale=w_scales, start=True, stop=True,
                 )
-            copy(y[:, rows, :], result[:])
+            copy(y[:, rows, :].rearrange("p t (n h) -> p t n h", h=HALVES), result[:].rearrange("p t (h n) -> p t n h", h=HALVES))
             if rows.start != 2:
                 stored = slice(0, 2) if rows.start == 0 else slice(2, 4)
                 nc.sync.dma_start(out_rows[:, stored, :], y[:, stored, :])

from contextlib import ExitStack

import concourse.mybir as mybir
from concourse.masks import make_identity

D, T, I, Q, E, G = 512, 2048, 512, 256, 512, 64
FLOPS = 2 * D * Q * I + 2 * I * E * Q

F32 = mybir.dt.float32
BF16 = mybir.dt.bfloat16
I32 = mybir.dt.int32
U32 = mybir.dt.uint32
U16 = mybir.dt.uint16
U8 = mybir.dt.uint8
FP8X4 = mybir.dt.float8_e4m3fn_x4
FP4X4 = mybir.dt.float4_e2m1fn_x4
ALU = mybir.AluOpType
ACT = mybir.ActivationFunctionType
AX = mybir.AxisListType

P = 128
PACK = 4
HALVES = Q // P
GROUP = I // G


def tile_attend_nearbest_pl_kernel(tc, query, keys_words, keys_scales, sharp, size, vals, offs, out_0, out_1, out_2):
    nc = tc.nc
    with ExitStack() as ctx:
        sb = ctx.enter_context(tc.tile_pool(name="sb", bufs=1))
        ps = ctx.enter_context(tc.psum_pool(name="ps", bufs=1))

        def alloc(name, shape, dtype, tag=None):
            return sb.tile(shape, dtype, name=name, tag=tag or name, align_bytes=64)

        offsets = sb.tile([P, I // 16], U16, name="offsets")
        nc.sync.dma_start(offsets[:], offs)
        key_scale_pool = alloc("key_scale_pool", [P, T], U8)
        nc.gpsimd.memset(key_scale_pool[:, : T // 2].bitcast(I32), 0)
        nc.vector.memset(key_scale_pool[:, T // 2 :].bitcast(I32), 0)
        key_word_pool = alloc("key_word_pool", [P, T], U16)
        nc.sync.dma_start(key_word_pool[:].bitcast(I32), keys_words[0].bitcast(I32))
        for quad in range(4):
            nc.sync.dma_start(
                key_scale_pool[32 * quad : 32 * quad + 4, :].bitcast(I32),
                keys_scales[0, 4 * quad : 4 * quad + 4, :].bitcast(I32),
            )
        q_raw = alloc("q_raw", [P, PACK, Q], F32)
        nc.sync.dma_start(q_raw[:], query.rearrange("(p t) q -> p t q", t=PACK))
        val_rows = vals.rearrange("(p t) n -> t p n", t=PACK)
        val_pool = [alloc("val_pool%d" % t, [P, T], F32) for t in range(PACK)]
        sharp_sb = alloc("sharp_sb", [P, HALVES], F32)
        nc.sync.dma_start(sharp_sb[:], sharp.rearrange("(p h) o -> p (h o)", h=HALVES))
        nc.sync.dma_start(val_pool[0][:], val_rows[0])
        size_sb = alloc("size_sb", [P, PACK], F32)
        nc.sync.dma_start(size_sb[:], size.rearrange("o (p t) -> p (o t)", t=PACK))
        for t in range(1, PACK):
            nc.sync.dma_start(val_pool[t][:], val_rows[t])

        ident = alloc("ident", [P, P], F32)
        make_identity(nc, ident[:])
        warm = alloc("warm", [P, 1], F32)
        nc.vector.memset(warm[:], 0.0)
        warm_out = alloc("warm_out", [P, 1], F32)
        nc.scalar.activation(warm_out[:], warm[:], ACT.Exp)
        one_less = alloc("one_less", [P, HALVES], F32)
        nc.gpsimd.tensor_scalar(one_less[:], sharp_sb[:], -1.0, 1.0, ALU.mult, ALU.add)

        size_rows = ps.tile([P, PACK, P], F32, name="size_rows", tag="size_rows")
        for t in range(PACK):
            nc.tensor.transpose(size_rows[:, t, :], size_sb[:, t : t + 1].to_broadcast([P, P]), ident[:])

        key_words = alloc("key_words", [P, I], U16)
        nc.vector.tensor_copy(key_words[:], key_word_pool[:].indirect(offsets[:]))
        key_scales = alloc("key_scales", [P, I], U8)
        nc.vector.tensor_copy(key_scales[:], key_scale_pool[:].indirect(offsets[:]))

        copy_out = (nc.vector.tensor_copy, nc.scalar.copy)
        q_bf = [alloc("q_bf%d" % h, [P, P, PACK], BF16) for h in range(HALVES)]
        for h in range(HALVES):
            nc.scalar.copy(
                q_bf[h][:].rearrange("p (c j) t -> p c t j", j=2),
                q_raw[:].rearrange("p t (c j h) -> p h c t j", j=2, h=HALVES)[:, h],
            )
        q_codes = alloc("q_codes", [P, Q], U32)
        q_scales = alloc("q_scales", [P, Q], U8)
        scores = []
        for h in range(HALVES):
            cols = slice(h * P, (h + 1) * P)
            nc.vector.quantize_mx(q_codes[:, cols].bitcast(FP8X4), q_scales[:, cols], q_bf[h][:].rearrange("p c t -> p (c t)"))
            a = ps.tile([P, I], F32, name="a%d" % h, tag="a%d" % h)
            nc.tensor.matmul_mx(
                a[:], lhsT=q_codes[:, cols].bitcast(FP8X4), lhsT_scale=q_scales[:, cols],
                rhs=key_words[:].bitcast(FP4X4), rhs_scale=key_scales[:], start=True, stop=True,
            )
            scores.append(a)
        val0_bf = alloc("val0_bf", [P, T], BF16)
        nc.scalar.activation(val0_bf[:], val_pool[0][:], ACT.Copy)

        best = alloc("best", [P, HALVES, G], F32)
        shift = [alloc("shift%d" % h, [P, G], F32) for h in range(HALVES)]
        neg_top = alloc("neg_top", [P, HALVES], F32)
        expo = [alloc("expo%d" % h, [P, G, GROUP], F32) for h in range(HALVES)]
        prob = [alloc("prob%d" % h, [P, I], F32) for h in range(HALVES)]
        total = [alloc("total%d" % h, [P, 1], F32) for h in range(HALVES)]
        inv = [alloc("inv%d" % h, [P, 1], F32) for h in range(HALVES)]
        for h in range(HALVES):
            nc.vector.tensor_reduce(best[:, h, :], scores[h][:].rearrange("p (g j) -> p g j", j=GROUP), AX.X, ALU.max)
        for h in range(HALVES):
            nc.gpsimd.tensor_scalar(shift[h][:], best[:, h, :], one_less[:, h : h + 1], 0.0, ALU.mult, ALU.add)
        for h in range(HALVES):
            nc.vector.scalar_tensor_tensor(
                expo[h][:], scores[h][:].rearrange("p (g j) -> p g j", j=GROUP), sharp_sb[:, h : h + 1],
                shift[h][:].unsqueeze(2).to_broadcast([P, G, GROUP]), ALU.mult, ALU.add,
            )
            if h == 0:
                nc.vector.tensor_reduce(neg_top[:], best[:], AX.X, ALU.max, negate=True)
            nc.scalar.activation(
                prob[h][:], expo[h][:].rearrange("p g j -> p (g j)"), ACT.Exp, bias=neg_top[:, h : h + 1], accum_out=total[h][:]
            )


        def turn(grouped, rows_bf, bank):
            words = rows_bf[:].bitcast(F32)
            for u in range(2):
                nc.tensor.transpose(bank[:, u, :], words[:, u : I // 2 : 2], ident[:])
            nc.scalar.copy(grouped.bitcast(F32).rearrange("p (r u) -> p r u", u=2), bank[:, 0:2, :].rearrange("p u r -> p r u"))

        def gather_values(t):
            v_bf = alloc("v_bf%d" % t, [P, I], BF16, ("expo1", "shift1", "prob1", "val_pool2")[t])
            if t == 0:
                nc.scalar.activation(v_bf[:], val0_bf[:].indirect(offsets[:]), ACT.Copy)
            else:
                nc.vector.tensor_copy(v_bf[:], val_pool[t][:].indirect(offsets[:]))
            return v_bf

        def turn_values(grouped, v_bf):
            turn(grouped, v_bf, ps.tile([P, PACK, P], F32, name="v_bank", tag="v_bank", bufs=2))

        first_values = gather_values(0)
        early = alloc("early", [P, 4 * I], BF16, "val0_bf")
        late = [alloc("late%d" % t, [P, I], BF16) for t in (2, 3)]
        turn_values(early[:, 3 * I : 4 * I], gather_values(1))
        for h in range(HALVES):
            nc.vector.reciprocal(inv[h][:], total[h][:])
        for h in range(HALVES):
            w_bf = alloc("w_bf%d" % h, [P, I], BF16)
            nc.vector.scalar_tensor_tensor(
                w_bf[:].rearrange("p (n t) -> p n t", t=PACK), prob[h][:].rearrange("p (n t) -> p n t", t=PACK), inv[h][:],
                size_rows[:].rearrange("p t n -> p n t"), ALU.mult, ALU.mult,
            )
            bank = ps.tile([P, PACK, P], F32, name="w_bank", tag="a%d" % h)
            turn(early[:, h * I : (h + 1) * I], w_bf, bank)
        turn(early[:, 2 * I : 3 * I], first_values, ps.tile([P, PACK, P], F32, name="v0_bank", tag="size_rows"))
        turn_values(late[0][:], gather_values(2))
        turn_values(late[1][:], gather_values(3))
        codes = alloc("codes", [P, 6 * P], U32, "val_pool3")
        scales = alloc("scales", [P, 6 * P], U8)
        for first, grouped in ((0, early), (4, late[0]), (5, late[1])):
            cols = slice(first * P, first * P + grouped.shape[1] // PACK)
            nc.vector.quantize_mx(codes[:, cols].bitcast(FP8X4), scales[:, cols], grouped[:])
        w_codes, w_scales = codes[:, :Q].bitcast(FP8X4), scales[:, :Q]

        y = alloc("y", [P, PACK, Q], F32)
        out_rows = out_0.rearrange("(p t) q -> p t q", t=PACK)
        for rows, copy in ((slice(0, 2), nc.scalar.copy), (slice(2, 3), nc.vector.tensor_copy), (slice(3, 4), nc.scalar.copy)):
            result = ps.tile([P, rows.stop - rows.start, Q], F32, name="result%d" % rows.start)
            for t in range(rows.start, rows.stop):
                cols = slice(Q + t * P, Q + (t + 1) * P)
                nc.tensor.matmul_mx(
                    result[:, t - rows.start, :], lhsT=codes[:, cols].bitcast(FP8X4), lhsT_scale=scales[:, cols],
                    rhs=w_codes, rhs_scale=w_scales, start=True, stop=True,
                )
            copy(y[:, rows, :].rearrange("p t (n h) -> p t n h", h=HALVES), result[:].rearrange("p t (h n) -> p t n h", h=HALVES))
            if rows.start != 2:
                stored = slice(0, 2) if rows.start == 0 else slice(2, 4)
                nc.sync.dma_start(out_rows[:, stored, :], y[:, stored, :])
        y_codes = alloc("y_codes", [P, Q], U32)
        y_scales = alloc("y_scales", [P, Q], U8)
        y_bf = [alloc("y_bf%d" % h, [P, P, PACK], BF16) for h in range(HALVES)]
        for h in range(HALVES):
            copy_out[h](
                y_bf[h][:].rearrange("p (c j) t -> p c t j", j=4),
                y[:, :, h * P : (h + 1) * P].rearrange("p t (c j) -> p c t j", j=4),
            )
        for h in range(HALVES):
            cols = slice(h * P, (h + 1) * P)
            nc.vector.quantize_mx(y_codes[:, cols].bitcast(FP8X4), y_scales[:, cols], y_bf[h][:].rearrange("p q t -> p (q t)"))
        nc.sync.dma_start(out_1[0].rearrange("p c r -> p (c r)").bitcast(I32), y_codes[:].bitcast(I32))
        for quad in range(4):
            queue = nc.sync if quad % 2 else nc.scalar
            queue.dma_start(out_2[0, 4 * quad : 4 * quad + 4, :].bitcast(I32), y_scales[32 * quad : 32 * quad + 4, :].bitcast(I32))
